import numpy as np
import ml_dtypes


def mxq(x, axis, fmt="e4m3"):
    dtype, down = {"e4m3": (ml_dtypes.float8_e4m3fn, 7), "e5m2": (ml_dtypes.float8_e5m2, 14)}[fmt]
    v = np.moveaxis(np.asarray(x, np.float32).astype(ml_dtypes.bfloat16).astype(np.float64), axis, -1)
    blocks = v.reshape(v.shape[:-1] + (-1, 32))
    amax = np.abs(blocks).max(-1, keepdims=True)
    byte = np.maximum(np.where(amax > 0, np.frexp(amax)[1] - 1 + 127, 0) - down, 1)
    scale = np.exp2(byte - 127.0)
    codes = (blocks / scale).astype(np.float32).astype(dtype).astype(np.float64)
    return np.moveaxis((codes * scale).reshape(v.shape), -1, axis)


WIDE = False


def mx_kscale(k):
    if not WIDE:
        return np.ones(k)
    levels = np.array([10, -10, 5, -5, 0])
    if k % 512:
        return np.exp2(np.random.permutation(np.resize(levels, k // 32))).repeat(32)
    a = np.empty((k // 512, 16))
    for p in range(k // 512):
        a[p, :8] = np.random.permutation(np.resize(levels, 8))
        for g in range(8):
            far = levels[np.abs(levels - a[p, g]) >= 10]
            a[p, g + 8] = far[np.random.randint(len(far))]
    return np.exp2(a.ravel()).repeat(32)


def f64(x):
    return np.asarray(x).astype(np.float64)


def striped(idx):
    return np.tile(idx.reshape(-1, 16).T, (8, 1)).astype(np.uint16)


def unstriped(offs):
    return offs[:16].T.reshape(-1).astype(np.int64)


E2M1 = np.array([0.0, 0.5, 1.0, 1.5, 2.0, 3.0, 4.0, 6.0, -0.0, -0.5, -1.0, -1.5, -2.0, -3.0, -4.0, -6.0])


def pack_weight(w, fmt):
    k, n = w.shape
    w = f64(np.asarray(w, np.float32).astype(ml_dtypes.bfloat16)).reshape(k // 32, 32, n)
    amax = np.abs(w).max(1)
    if fmt == "e4m3":
        byte = np.frexp(amax)[1] - 1 + 127 - 7
    else:
        mant, ex = np.frexp(amax / 6.0)
        byte = np.where(mant > 0.5, ex, ex - 1) + 127
    byte = np.clip(np.where(amax > 0, byte, 1), 1, 254)
    scaled = (w * np.exp2(127.0 - byte)[:, None, :]).reshape(k, n).astype(np.float32)
    by_word = np.ascontiguousarray(scaled.reshape(k // 512, 128, 4, n).transpose(0, 1, 3, 2))
    if fmt == "e4m3":
        words = by_word.astype(ml_dtypes.float8_e4m3fn).view(np.uint8)
    else:
        c = by_word.astype(ml_dtypes.float4_e2m1fn).view(np.uint8) & 0xF
        words = (c[..., 0::2] | (c[..., 1::2] << 4)).reshape(k // 512, 128, 2 * n)
    return np.ascontiguousarray(words), np.ascontiguousarray(byte.astype(np.uint8).reshape(k // 512, 16, n))


def unpack_weight(words, scales, fmt):
    g, _, n = scales.shape
    words = np.ascontiguousarray(words).reshape(g, 128, n, -1)
    if fmt == "e4m3":
        vals = words.view(ml_dtypes.float8_e4m3fn).astype(np.float64)
    else:
        nib = np.empty((g, 128, n, 4), np.uint8)
        nib[..., 0::2] = words & 0xF
        nib[..., 1::2] = words >> 4
        vals = E2M1[nib]
    vals = vals * np.repeat(np.exp2(scales.astype(np.float64) - 127.0), 8, axis=1)[..., None]
    return vals.transpose(0, 1, 3, 2).reshape(g * 512, n)


def silu(v):
    return v / (1.0 + np.exp(-np.maximum(v, -700.0)))


K, T, E, C, N = 1024, 640, 20, 128, 128
TOP = 4


def by_expert(wq, xq):
    return np.concatenate([wq[e].T @ xq[:, e * C:(e + 1) * C] for e in range(E)], axis=1)


def setup_inputs():
    n = np.random.standard_normal
    s = mx_kscale(K)[:, None]
    deal = np.repeat(np.arange(E), C).reshape(TOP, T)[:, np.random.permutation(T)]
    deal = np.take_along_axis(deal, np.argsort(np.random.rand(TOP, T), axis=0), axis=0)
    for _ in range(8):
        s_, t_ = np.random.permutation(T).reshape(2, -1); r = np.random.randint(TOP, size=T // 2); x, y = deal[r, s_].copy(), deal[r, t_].copy()
        ok = ~((deal[:, s_] == y).any(0) | (deal[:, t_] == x).any(0)); deal[r[ok], s_[ok]] = y[ok]; deal[r[ok], t_[ok]] = x[ok]
    order = np.lexsort((np.random.rand(TOP * T), deal.reshape(-1)))
    slot_token = order % T; pos = np.empty(TOP * T, np.int64); pos[order] = np.arange(TOP * T); pos = pos.reshape(TOP, T)
    g = np.random.uniform(0.5, 1.5, (TOP, T)); g = g / g.sum(0)
    x = pack_weight(n((K, T)) * s, "e4m3")
    return {
        "x_words": x[0],
        "x_scales": x[1],
        "w": (n((E + 1, K, N)) / np.sqrt(K) / s[None]).astype(np.float32),
        "b": (0.3 * n((N, E + 1))).astype(np.float32),
        "gate": np.stack([np.tile(r, (N, 1)) for r in g]).astype(np.float32),
        "offs": striped(slot_token),
        "pos1": striped(pos[0]),
        "pos2": striped(pos[1]),
        "pos3": striped(pos[2]),
        "pos4": striped(pos[3]),
    }


def reference(x_words, x_scales, w, b, gate, offs, pos1, pos2, pos3, pos4):
    idx = unstriped(offs)
    wq = mxq(f64(w), 1, "e4m3")
    xs = unpack_weight(x_words, x_scales, "e4m3")
    ys = silu((wq[E].T @ xs) + f64(b)[:, E:])
    xq = unpack_weight(x_words, x_scales, "e4m3")[:, idx]
    y = by_expert(wq, xq)
    y = silu(y + np.repeat(f64(b)[:, :E], C, axis=1))
    return ys + sum(f64(gate[r]) * y[:, unstriped(p)] for r, p in enumerate((pos1, pos2, pos3, pos4)))

@@ -1,0 +1,269 @@
+from contextlib import ExitStack
+
+import concourse.mybir as mybir
+from concourse.masks import make_identity
+
+K, T, E, C, N = 1024, 640, 20, 128, 128
+TOP = 4
+FLOPS = 2 * K * N * (E * C + T)
+
+F32 = mybir.dt.float32
+BF16 = mybir.dt.bfloat16
+I32 = mybir.dt.int32
+U32 = mybir.dt.uint32
+U16 = mybir.dt.uint16
+U8 = mybir.dt.uint8
+FP8X4 = mybir.dt.float8_e4m3fn_x4
+SILU = mybir.ActivationFunctionType.Silu
+MULT = mybir.AluOpType.mult
+ADD = mybir.AluOpType.add
+
+P = 128
+PACK = 4
+PASSES = 2
+WINDOW = 704
+GROUP = 4
+GROUPS = E // GROUP
+SLOTS = GROUP * C
+LOADS = [[0], [1], [2], [3], [4, 5], [6, 7], [8, 9], [10, 11], [12], [13], [14], [15], [16], [17], [18], [19]]
+EARLY = 14
+COPY = mybir.ActivationFunctionType.Copy
+QUANT = [[0, 1], [2, 3], [4, 5], [6, 7], [8, 9], [10, 11], [12, 13], [14, 15], [16], [17], [18], [19], [20]]
+VECTOR_CASTS = (17, 18, 20)
+SPLIT = 384
+
+
+def tile_moe_shr_lin_silu_kernel(
+    tc, x_words, x_scales, w, b, gate, offs, pos1, pos2, pos3, pos4, out
+):
+    nc = tc.nc
+    with ExitStack() as ctx:
+        keep = ctx.enter_context(tc.tile_pool(name="keep", bufs=1))
+        psum = ctx.enter_context(tc.psum_pool(name="psum", bufs=6))
+        psum_s = ctx.enter_context(tc.psum_pool(name="psum_s", bufs=1))
+
+        slot_token = keep.tile([P, E * C // 16], U16, name="slot_token")
+        token_slot = [keep.tile([P, T // 16], U16, name="token_slot%d" % r) for r in range(TOP)]
+        words = [keep.tile([P, WINDOW], I32, name="words%d" % o, align_bytes=64) for o in range(PASSES)]
+        scales = keep.tile([P, WINDOW], U8, name="scales", align_bytes=64)
+        bias = keep.tile([P, E + 1], F32, name="bias")
+        gates = [keep.tile([P, T], F32, name="gate%d" % r) for r in range(TOP)]
+
+        nc.vector.memset(scales[:].bitcast(I32), 0)
+        for o in range(PASSES):
+            nc.vector.memset(words[o][:, T:], 0)
+
+        identity = keep.tile([P, P], F32, name="identity")
+        make_identity(nc, identity[:])
+
+        raw = {}
+
+        def load_words(o):
+            (nc.sync if o else nc.scalar).dma_start(
+                out=words[o][:, :T], in_=x_words[o].rearrange("p t r -> p (t r)").bitcast(I32)
+            )
+
+        def load_weights(experts, split):
+            first, count = experts[0], len(experts)
+            t = keep.tile([P, count * PASSES, PACK * N], F32, name="raw%d" % first, align_bytes=64)
+            src = w[first : first + count].rearrange("e (o p r) n -> p (e o) (r n)", o=PASSES, r=PACK)
+            if split:
+                for o in range(PASSES):
+                    nc.sync.dma_start(out=t[:, o, :], in_=src[:, o, :])
+            else:
+                nc.sync.dma_start(out=t[:], in_=src)
+            for i, e in enumerate(experts):
+                raw[e] = t[:, PASSES * i : PASSES * (i + 1), :]
+
+        nc.sync.dma_start(slot_token[:], offs)
+        load_words(0)
+        for q in range(4):
+            nc.scalar.dma_start(
+                out=scales[32 * q : 32 * q + 8, :T].bitcast(I32),
+                in_=x_scales[:, 4 * q : 4 * q + 4, :].bitcast(I32),
+            )
+        load_weights(LOADS[0], False)
+        load_words(1)
+        load_weights(LOADS[1], False)
+        nc.sync.dma_start(out=bias[:], in_=b)
+        for experts in LOADS[2:8]:
+            load_weights(experts, False)
+        for r, pos in enumerate((pos1, pos2, pos3, pos4)):
+            nc.sync.dma_start(token_slot[r][:], pos)
+        for experts in LOADS[8:-1]:
+            load_weights(experts, False)
+        load_weights(LOADS[-1], True)
+        load_weights([E], False)
+        for r in range(TOP):
+            nc.sync.dma_start(out=gates[r][:], in_=gate[r])
+
+        slot_words = {}
+        slot_scales = {}
+
+        def gather_words(g, o):
+            t = keep.tile([P, SLOTS], U32, name="slot_words%d_%d" % (g, o), align_bytes=64)
+            entries = slot_token[:, g * SLOTS // 16 : (g + 1) * SLOTS // 16]
+            nc.vector.tensor_copy(t[:], words[o][:].bitcast(U32).indirect(entries))
+            slot_words[g, o] = t
+
+        def gather_scales(g):
+            t = keep.tile([P, SLOTS], U8, name="slot_scales%d" % g, align_bytes=64)
+            entries = slot_token[:, g * SLOTS // 16 : (g + 1) * SLOTS // 16]
+            nc.vector.tensor_copy(t[:], scales[:].indirect(entries))
+            slot_scales[g] = t
+
+        y = keep.tile([P, E * C], F32, name="y")
+        ys = keep.tile([P, T], F32, name="ys")
+        rounded = {}
+        codes = {}
+        w_scales = {}
+
+        def cast(j, only=None):
+            experts = QUANT[j]
+            t = rounded[j] if j in rounded else keep.tile([P, len(experts), PASSES * N * PACK], BF16, name="rounded%d" % j,
+                          tag="rounded%d" % min(j, len(QUANT) - 2), align_bytes=64)
+            rounded[j] = t
+            for i, e in enumerate(experts):
+                if only is not None and e not in only:
+                    continue
+                dst = t[:, i, :].rearrange("p (o c i r) -> p o c r i", o=PASSES, i=4, r=PACK)
+                src = raw[e].rearrange("p o (r c i) -> p o c r i", r=PACK, i=4)
+                if e == 0:
+                    for o in range(PASSES):
+                        nc.scalar.activation(out=dst[:, o], in_=src[:, o], func=COPY)
+                elif e == E - 1:
+                    nc.scalar.copy(out=dst[:, 0], in_=src[:, 0])
+                    nc.vector.tensor_copy(out=dst[:, 1], in_=src[:, 1])
+                elif e in VECTOR_CASTS:
+                    nc.vector.tensor_copy(out=dst, in_=src)
+                else:
+                    nc.scalar.copy(out=dst, in_=src)
+
+        def quantize(j):
+            experts = QUANT[j]
+            width = len(experts) * PASSES * N
+            cd = keep.tile([P, width], U32, name="codes%d" % j, align_bytes=64)
+            if experts[0] < EARLY:
+                sc = early_scales[:, experts[0] * PASSES * N : (experts[-1] + 1) * PASSES * N]
+            else:
+                sc = keep.tile([P, width], U8, name="w_scales%d" % j, align_bytes=64)
+            nc.vector.quantize_mx(
+                out=cd[:].bitcast(FP8X4), scales=sc[:], in_=rounded[j][:].rearrange("p e x -> p (e x)")
+            )
+            for i, e in enumerate(experts):
+                codes[e] = cd[:, i * PASSES * N : (i + 1) * PASSES * N]
+                w_scales[e] = sc[:, i * PASSES * N : (i + 1) * PASSES * N]
+
+        def product(acc, e, rhs, rhs_scales, cols):
+            for o in range(PASSES):
+                nc.tensor.matmul_mx(
+                    out=acc,
+                    lhsT=codes[e][:, o * N : (o + 1) * N].bitcast(FP8X4),
+                    lhsT_scale=w_scales[e][:, o * N : (o + 1) * N],
+                    rhs=rhs[o][:, cols].bitcast(FP8X4),
+                    rhs_scale=rhs_scales[4 * o :, cols],
+                    start=(o == 0),
+                    stop=(o == PASSES - 1),
+                )
+
+        def expert(e):
+            g, c = divmod(e, GROUP)
+            bank = psum.tile([P, 512], F32, name="bank")
+            cols = slice(c * C, (c + 1) * C)
+            product(bank[:, :C], e, [slot_words[g, o] for o in range(PASSES)], slot_scales[g], cols)
+            nc.scalar.activation(
+                out=y[:, e * C : (e + 1) * C], in_=bank[:, :C], func=SILU, bias=bias[:, e : e + 1]
+            )
+
+        def shared():
+            for i, cols in enumerate((slice(0, 512), slice(512, T))):
+                bank = psum_s.tile([P, 512], F32, name="shared_bank%d" % i)
+                width = cols.stop - cols.start
+                product(bank[:, :width], E, words, scales, cols)
+                nc.scalar.activation(
+                    out=ys[:, cols], in_=bank[:, :width], func=SILU, bias=bias[:, E : E + 1]
+                )
+
+        def finish(j):
+            quantize(j)
+            for e in QUANT[j]:
+                expert(e)
+
+        gather_words(0, 0)
+        gather_words(1, 0)
+        gather_words(0, 1)
+        gather_scales(0)
+        gather_words(1, 1)
+        gather_scales(1)
+        for g in range(2, GROUPS):
+            gather_words(g, 0)
+            gather_words(g, 1)
+            gather_scales(g)
+        for j in range(0, 7):
+            cast(j)
+        early_scales = keep.tile(
+            [P, EARLY * PASSES * N], U8, name="early_scales", tag="raw%d" % (EARLY - 2), align_bytes=64
+        )
+        cast(7, [14])
+        finish(0)
+        finish(1)
+        cast(7, [15])
+        finish(2)
+        finish(3)
+        cast(8)
+        for j in (4, 5, 6):
+            finish(j)
+        cast(9)
+        finish(7)
+        cast(10)
+        cast(11)
+        finish(8)
+        finish(9)
+        finish(10)
+        finish(11)
+        cast(12)
+        quantize(12)
+        shared()
+
+        z = [keep.tile([P, T], F32, name="z%d" % r) for r in range(TOP)]
+        turned = keep.tile([P, T], F32, name="turned")
+        total = keep.tile([P, T], F32, name="total")
+        blocks = [slice(i * P, (i + 1) * P) for i in range(T // P)]
+        sums = [psum.tile([P, 512], F32, name="bank") for i in range(T // P)]
+
+        def fetch(r, cols):
+            entries = token_slot[r][:, cols.start // 16 : cols.stop // 16]
+            nc.vector.tensor_tensor(z[r][:, cols], y[:].indirect(entries), gates[r][:, cols], MULT)
+
+        def add_turned(term, cols, start, stop):
+            for i in range(cols.start // P, cols.stop // P):
+                nc.tensor.matmul(
+                    sums[i][:, :P], lhsT=term[:, blocks[i]], rhs=identity[:],
+                    start=start, stop=stop, is_transpose=True,
+                )
+
+        whole = slice(0, T)
+        halves = (slice(0, SPLIT), slice(SPLIT, T))
+        fetch(0, whole)
+        add_turned(z[0], whole, True, False)
+        add_turned(ys, whole, False, False)
+        fetch(1, whole)
+        add_turned(z[1], whole, False, False)
+        partial = []
+        for h, cols in enumerate(halves):
+            fetch(2, cols)
+            add_turned(z[2], cols, False, True)
+            back = psum_s.tile([P, 512], F32, name="shared_bank%d" % h)
+            partial.append(back)
+            for i in range(cols.start // P, cols.stop // P):
+                nc.scalar.copy(out=turned[:, blocks[i]], in_=sums[i][:, :P])
+                nc.tensor.transpose(
+                    back[:, i * P - cols.start : (i + 1) * P - cols.start], turned[:, blocks[i]], identity[:]
+                )
+        for cols in halves:
+            fetch(3, cols)
+        for h, cols in enumerate(halves):
+            nc.vector.tensor_tensor(
+                total[:, cols], partial[h][:, : cols.stop - cols.start], z[3][:, cols], ADD
+            )
+            nc.sync.dma_start(out=out[:, cols], in_=total[:, cols])

@@ -25,12 +25,12 @@ WINDOW = 704
 GROUP = 4
 GROUPS = E // GROUP
 SLOTS = GROUP * C
-LOADS = [[0], [1], [2], [3], [4, 5], [6, 7], [8, 9], [10, 11], [12], [13], [14], [15], [16], [17], [18], [19]]
-EARLY = 14
+LOADS = [[e] for e in range(E)]
 COPY = mybir.ActivationFunctionType.Copy
-QUANT = [[0, 1], [2, 3], [4, 5], [6, 7], [8, 9], [10, 11], [12, 13], [14, 15], [16], [17], [18], [19], [20]]
-VECTOR_CASTS = (17, 18, 20)
+QUANT = [[e, e + 1] for e in range(0, E, 2)] + [[E]]
+VECTOR_CASTS = (17, 18, 19, 20)
 SPLIT = 384
+ROUNDED_TAG = {10: "rounded9"}
 
 
 def tile_moe_shr_lin_silu_kernel(
@@ -53,13 +53,10 @@ def tile_moe_shr_lin_silu_kernel(
         for o in range(PASSES):
             nc.vector.memset(words[o][:, T:], 0)
 
-        identity = keep.tile([P, P], F32, name="identity")
-        make_identity(nc, identity[:])
-
         raw = {}
 
         def load_words(o):
-            (nc.sync if o else nc.scalar).dma_start(
+            nc.sync.dma_start(
                 out=words[o][:, :T], in_=x_words[o].rearrange("p t r -> p (t r)").bitcast(I32)
             )
 
@@ -75,23 +72,22 @@ def tile_moe_shr_lin_silu_kernel(
             for i, e in enumerate(experts):
                 raw[e] = t[:, PASSES * i : PASSES * (i + 1), :]
 
+        small = [
+            (scales[32 * q : 32 * q + 8, :T].bitcast(I32), x_scales[:, 4 * q : 4 * q + 4, :].bitcast(I32))
+            for q in range(4)
+        ]
+        small += [(bias[:], b)]
+        small += [(token_slot[r][:], pos) for r, pos in enumerate((pos1, pos2, pos3, pos4))]
         nc.sync.dma_start(slot_token[:], offs)
         load_words(0)
-        for q in range(4):
-            nc.scalar.dma_start(
-                out=scales[32 * q : 32 * q + 8, :T].bitcast(I32),
-                in_=x_scales[:, 4 * q : 4 * q + 4, :].bitcast(I32),
-            )
         load_weights(LOADS[0], False)
         load_words(1)
-        load_weights(LOADS[1], False)
-        nc.sync.dma_start(out=bias[:], in_=b)
-        for experts in LOADS[2:8]:
-            load_weights(experts, False)
-        for r, pos in enumerate((pos1, pos2, pos3, pos4)):
-            nc.sync.dma_start(token_slot[r][:], pos)
-        for experts in LOADS[8:-1]:
-            load_weights(experts, False)
+        identity = keep.tile([P, P], F32, name="identity")
+        make_identity(nc, identity[:])
+        for e in range(1, E - 1):
+            load_weights(LOADS[e], False)
+            if 2 <= e < 2 + len(small):
+                nc.sync.dma_start(*small[e - 2])
         load_weights(LOADS[-1], True)
         load_weights([E], False)
         for r in range(TOP):
@@ -100,10 +96,9 @@ def tile_moe_shr_lin_silu_kernel(
         slot_words = {}
         slot_scales = {}
 
-        def gather_words(g, o):
-            t = keep.tile([P, SLOTS], U32, name="slot_words%d_%d" % (g, o), align_bytes=64)
+        def gather_words(g, o, t):
             entries = slot_token[:, g * SLOTS // 16 : (g + 1) * SLOTS // 16]
-            nc.vector.tensor_copy(t[:], words[o][:].bitcast(U32).indirect(entries))
+            nc.vector.tensor_copy(t, words[o][:].bitcast(U32).indirect(entries))
             slot_words[g, o] = t
 
         def gather_scales(g):
@@ -112,7 +107,6 @@ def tile_moe_shr_lin_silu_kernel(
             nc.vector.tensor_copy(t[:], scales[:].indirect(entries))
             slot_scales[g] = t
 
-        y = keep.tile([P, E * C], F32, name="y")
         ys = keep.tile([P, T], F32, name="ys")
         rounded = {}
         codes = {}
@@ -121,7 +115,7 @@ def tile_moe_shr_lin_silu_kernel(
         def cast(j, only=None):
             experts = QUANT[j]
             t = rounded[j] if j in rounded else keep.tile([P, len(experts), PASSES * N * PACK], BF16, name="rounded%d" % j,
-                          tag="rounded%d" % min(j, len(QUANT) - 2), align_bytes=64)
+                          tag=ROUNDED_TAG.get(j, "rounded%d" % j), align_bytes=64)
             rounded[j] = t
             for i, e in enumerate(experts):
                 if only is not None and e not in only:
@@ -132,8 +126,9 @@ def tile_moe_shr_lin_silu_kernel(
                     for o in range(PASSES):
                         nc.scalar.activation(out=dst[:, o], in_=src[:, o], func=COPY)
                 elif e == E - 1:
-                    nc.scalar.copy(out=dst[:, 0], in_=src[:, 0])
-                    nc.vector.tensor_copy(out=dst[:, 1], in_=src[:, 1])
+                    for o in range(PASSES):
+                        half = "p (h c) r i -> p h c r i"
+                        nc.vector.tensor_copy(out=dst[:, o].rearrange(half, h=2), in_=src[:, o].rearrange(half, h=2))
                 elif e in VECTOR_CASTS:
                     nc.vector.tensor_copy(out=dst, in_=src)
                 else:
@@ -143,10 +138,7 @@ def tile_moe_shr_lin_silu_kernel(
             experts = QUANT[j]
             width = len(experts) * PASSES * N
             cd = keep.tile([P, width], U32, name="codes%d" % j, align_bytes=64)
-            if experts[0] < EARLY:
-                sc = early_scales[:, experts[0] * PASSES * N : (experts[-1] + 1) * PASSES * N]
-            else:
-                sc = keep.tile([P, width], U8, name="w_scales%d" % j, align_bytes=64)
+            sc = keep.tile([P, width], U8, name="w_scales%d" % j, align_bytes=64)
             nc.vector.quantize_mx(
                 out=cd[:].bitcast(FP8X4), scales=sc[:], in_=rounded[j][:].rearrange("p e x -> p (e x)")
             )
@@ -189,40 +181,22 @@ def tile_moe_shr_lin_silu_kernel(
             for e in QUANT[j]:
                 expert(e)
 
-        gather_words(0, 0)
-        gather_words(1, 0)
-        gather_words(0, 1)
-        gather_scales(0)
-        gather_words(1, 1)
-        gather_scales(1)
+        all_words = keep.tile([P, GROUPS, PASSES, SLOTS], U32, name="all_words", align_bytes=64)
+        for o in range(PASSES):
+            for g in range(2):
+                gather_words(g, o, all_words[:, g, o, :])
         for g in range(2, GROUPS):
-            gather_words(g, 0)
-            gather_words(g, 1)
+            for o in range(PASSES):
+                gather_words(g, o, all_words[:, g, o, :])
+        for g in range(GROUPS):
             gather_scales(g)
-        for j in range(0, 7):
+        for j in range(len(QUANT) - 1):
             cast(j)
-        early_scales = keep.tile(
-            [P, EARLY * PASSES * N], U8, name="early_scales", tag="raw%d" % (EARLY - 2), align_bytes=64
-        )
-        cast(7, [14])
-        finish(0)
-        finish(1)
-        cast(7, [15])
-        finish(2)
-        finish(3)
-        cast(8)
-        for j in (4, 5, 6):
+        y = keep.tile([P, E * C], F32, name="y", tag="raw16", align_bytes=64)
+        for j in range(len(QUANT) - 1):
             finish(j)
-        cast(9)
-        finish(7)
-        cast(10)
-        cast(11)
-        finish(8)
-        finish(9)
-        finish(10)
-        finish(11)
-        cast(12)
-        quantize(12)
+        cast(len(QUANT) - 1)
+        quantize(len(QUANT) - 1)
         shared()
 
         z = [keep.tile([P, T], F32, name="z%d" % r) for r in range(TOP)]

@@ -28,7 +28,7 @@ SLOTS = GROUP * C
 LOADS = [[e] for e in range(E)]
 COPY = mybir.ActivationFunctionType.Copy
 QUANT = [[e, e + 1] for e in range(0, E, 2)] + [[E]]
-VECTOR_CASTS = (17, 18, 19, 20)
+VECTOR_CASTS = (16, 17, 18, 19, 20)
 SPLIT = 384
 ROUNDED_TAG = {10: "rounded9"}
 
@@ -77,7 +77,6 @@ def tile_moe_shr_lin_silu_kernel(
             for q in range(4)
         ]
         small += [(bias[:], b)]
-        small += [(token_slot[r][:], pos) for r, pos in enumerate((pos1, pos2, pos3, pos4))]
         nc.sync.dma_start(slot_token[:], offs)
         load_words(0)
         load_weights(LOADS[0], False)
@@ -90,7 +89,8 @@ def tile_moe_shr_lin_silu_kernel(
                 nc.sync.dma_start(*small[e - 2])
         load_weights(LOADS[-1], True)
         load_weights([E], False)
-        for r in range(TOP):
+        for r, pos in enumerate((pos1, pos2, pos3, pos4)):
+            nc.sync.dma_start(token_slot[r][:], pos)
             nc.sync.dma_start(out=gates[r][:], in_=gate[r])
 
         slot_words = {}
@@ -192,7 +192,7 @@ def tile_moe_shr_lin_silu_kernel(
             gather_scales(g)
         for j in range(len(QUANT) - 1):
             cast(j)
-        y = keep.tile([P, E * C], F32, name="y", tag="raw16", align_bytes=64)
+        y = keep.tile([P, E * C], F32, name="y", tag="raw15", align_bytes=64)
         for j in range(len(QUANT) - 1):
             finish(j)
         cast(len(QUANT) - 1)

from contextlib import ExitStack

import concourse.mybir as mybir
from concourse.masks import make_identity

K, T, E, C, N = 1024, 640, 20, 128, 128
TOP = 4
FLOPS = 2 * K * N * (E * C + T)

F32 = mybir.dt.float32
BF16 = mybir.dt.bfloat16
I32 = mybir.dt.int32
U32 = mybir.dt.uint32
U16 = mybir.dt.uint16
U8 = mybir.dt.uint8
FP8X4 = mybir.dt.float8_e4m3fn_x4
SILU = mybir.ActivationFunctionType.Silu
MULT = mybir.AluOpType.mult
ADD = mybir.AluOpType.add

P = 128
PACK = 4
PASSES = 2
WINDOW = 704
GROUP = 4
GROUPS = E // GROUP
SLOTS = GROUP * C
LOADS = [[e] for e in range(E)]
COPY = mybir.ActivationFunctionType.Copy
QUANT = [[e, e + 1] for e in range(0, E, 2)] + [[E]]
VECTOR_CASTS = (16, 17, 18, 19, 20)
SPLIT = 384
ROUNDED_TAG = {10: "rounded9"}


def tile_moe_shr_lin_silu_kernel(
    tc, x_words, x_scales, w, b, gate, offs, pos1, pos2, pos3, pos4, out
):
    nc = tc.nc
    with ExitStack() as ctx:
        keep = ctx.enter_context(tc.tile_pool(name="keep", bufs=1))
        psum = ctx.enter_context(tc.psum_pool(name="psum", bufs=6))
        psum_s = ctx.enter_context(tc.psum_pool(name="psum_s", bufs=1))

        slot_token = keep.tile([P, E * C // 16], U16, name="slot_token")
        token_slot = [keep.tile([P, T // 16], U16, name="token_slot%d" % r) for r in range(TOP)]
        words = [keep.tile([P, WINDOW], I32, name="words%d" % o, align_bytes=64) for o in range(PASSES)]
        scales = keep.tile([P, WINDOW], U8, name="scales", align_bytes=64)
        bias = keep.tile([P, E + 1], F32, name="bias")
        gates = [keep.tile([P, T], F32, name="gate%d" % r) for r in range(TOP)]

        nc.vector.memset(scales[:].bitcast(I32), 0)
        for o in range(PASSES):
            nc.vector.memset(words[o][:, T:], 0)

        raw = {}

        def load_words(o):
            nc.sync.dma_start(
                out=words[o][:, :T], in_=x_words[o].rearrange("p t r -> p (t r)").bitcast(I32)
            )

        def load_weights(experts, split):
            first, count = experts[0], len(experts)
            t = keep.tile([P, count * PASSES, PACK * N], F32, name="raw%d" % first, align_bytes=64)
            src = w[first : first + count].rearrange("e (o p r) n -> p (e o) (r n)", o=PASSES, r=PACK)
            if split:
                for o in range(PASSES):
                    nc.sync.dma_start(out=t[:, o, :], in_=src[:, o, :])
            else:
                nc.sync.dma_start(out=t[:], in_=src)
            for i, e in enumerate(experts):
                raw[e] = t[:, PASSES * i : PASSES * (i + 1), :]

        small = [
            (scales[32 * q : 32 * q + 8, :T].bitcast(I32), x_scales[:, 4 * q : 4 * q + 4, :].bitcast(I32))
            for q in range(4)
        ]
        small += [(bias[:], b)]
        nc.sync.dma_start(slot_token[:], offs)
        load_words(0)
        load_weights(LOADS[0], False)
        load_words(1)
        identity = keep.tile([P, P], F32, name="identity")
        make_identity(nc, identity[:])
        for e in range(1, E - 1):
            load_weights(LOADS[e], False)
            if 2 <= e < 2 + len(small):
                nc.sync.dma_start(*small[e - 2])
        load_weights(LOADS[-1], True)
        load_weights([E], False)
        for r, pos in enumerate((pos1, pos2, pos3, pos4)):
            nc.sync.dma_start(token_slot[r][:], pos)
            nc.sync.dma_start(out=gates[r][:], in_=gate[r])

        slot_words = {}
        slot_scales = {}

        def gather_words(g, o, t):
            entries = slot_token[:, g * SLOTS // 16 : (g + 1) * SLOTS // 16]
            nc.vector.tensor_copy(t, words[o][:].bitcast(U32).indirect(entries))
            slot_words[g, o] = t

        def gather_scales(g):
            t = keep.tile([P, SLOTS], U8, name="slot_scales%d" % g, align_bytes=64)
            entries = slot_token[:, g * SLOTS // 16 : (g + 1) * SLOTS // 16]
            nc.vector.tensor_copy(t[:], scales[:].indirect(entries))
            slot_scales[g] = t

        ys = keep.tile([P, T], F32, name="ys")
        rounded = {}
        codes = {}
        w_scales = {}

        def cast(j, only=None):
            experts = QUANT[j]
            t = rounded[j] if j in rounded else keep.tile([P, len(experts), PASSES * N * PACK], BF16, name="rounded%d" % j,
                          tag=ROUNDED_TAG.get(j, "rounded%d" % j), align_bytes=64)
            rounded[j] = t
            for i, e in enumerate(experts):
                if only is not None and e not in only:
                    continue
                dst = t[:, i, :].rearrange("p (o c i r) -> p o c r i", o=PASSES, i=4, r=PACK)
                src = raw[e].rearrange("p o (r c i) -> p o c r i", r=PACK, i=4)
                if e == 0:
                    for o in range(PASSES):
                        nc.scalar.activation(out=dst[:, o], in_=src[:, o], func=COPY)
                elif e == E - 1:
                    for o in range(PASSES):
                        half = "p (h c) r i -> p h c r i"
                        nc.vector.tensor_copy(out=dst[:, o].rearrange(half, h=2), in_=src[:, o].rearrange(half, h=2))
                elif e in VECTOR_CASTS:
                    nc.vector.tensor_copy(out=dst, in_=src)
                else:
                    nc.scalar.copy(out=dst, in_=src)

        def quantize(j):
            experts = QUANT[j]
            width = len(experts) * PASSES * N
            cd = keep.tile([P, width], U32, name="codes%d" % j, align_bytes=64)
            sc = keep.tile([P, width], U8, name="w_scales%d" % j, align_bytes=64)
            nc.vector.quantize_mx(
                out=cd[:].bitcast(FP8X4), scales=sc[:], in_=rounded[j][:].rearrange("p e x -> p (e x)")
            )
            for i, e in enumerate(experts):
                codes[e] = cd[:, i * PASSES * N : (i + 1) * PASSES * N]
                w_scales[e] = sc[:, i * PASSES * N : (i + 1) * PASSES * N]

        def product(acc, e, rhs, rhs_scales, cols):
            for o in range(PASSES):
                nc.tensor.matmul_mx(
                    out=acc,
                    lhsT=codes[e][:, o * N : (o + 1) * N].bitcast(FP8X4),
                    lhsT_scale=w_scales[e][:, o * N : (o + 1) * N],
                    rhs=rhs[o][:, cols].bitcast(FP8X4),
                    rhs_scale=rhs_scales[4 * o :, cols],
                    start=(o == 0),
                    stop=(o == PASSES - 1),
                )

        def expert(e):
            g, c = divmod(e, GROUP)
            bank = psum.tile([P, 512], F32, name="bank")
            cols = slice(c * C, (c + 1) * C)
            product(bank[:, :C], e, [slot_words[g, o] for o in range(PASSES)], slot_scales[g], cols)
            nc.scalar.activation(
                out=y[:, e * C : (e + 1) * C], in_=bank[:, :C], func=SILU, bias=bias[:, e : e + 1]
            )

        def shared():
            for i, cols in enumerate((slice(0, 512), slice(512, T))):
                bank = psum_s.tile([P, 512], F32, name="shared_bank%d" % i)
                width = cols.stop - cols.start
                product(bank[:, :width], E, words, scales, cols)
                nc.scalar.activation(
                    out=ys[:, cols], in_=bank[:, :width], func=SILU, bias=bias[:, E : E + 1]
                )

        def finish(j):
            quantize(j)
            for e in QUANT[j]:
                expert(e)

        all_words = keep.tile([P, GROUPS, PASSES, SLOTS], U32, name="all_words", align_bytes=64)
        for o in range(PASSES):
            for g in range(2):
                gather_words(g, o, all_words[:, g, o, :])
        for g in range(2, GROUPS):
            for o in range(PASSES):
                gather_words(g, o, all_words[:, g, o, :])
        for g in range(GROUPS):
            gather_scales(g)
        for j in range(len(QUANT) - 1):
            cast(j)
        y = keep.tile([P, E * C], F32, name="y", tag="raw15", align_bytes=64)
        for j in range(len(QUANT) - 1):
            finish(j)
        cast(len(QUANT) - 1)
        quantize(len(QUANT) - 1)
        shared()

        z = [keep.tile([P, T], F32, name="z%d" % r) for r in range(TOP)]
        turned = keep.tile([P, T], F32, name="turned")
        total = keep.tile([P, T], F32, name="total")
        blocks = [slice(i * P, (i + 1) * P) for i in range(T // P)]
        sums = [psum.tile([P, 512], F32, name="bank") for i in range(T // P)]

        def fetch(r, cols):
            entries = token_slot[r][:, cols.start // 16 : cols.stop // 16]
            nc.vector.tensor_tensor(z[r][:, cols], y[:].indirect(entries), gates[r][:, cols], MULT)

        def add_turned(term, cols, start, stop):
            for i in range(cols.start // P, cols.stop // P):
                nc.tensor.matmul(
                    sums[i][:, :P], lhsT=term[:, blocks[i]], rhs=identity[:],
                    start=start, stop=stop, is_transpose=True,
                )

        whole = slice(0, T)
        halves = (slice(0, SPLIT), slice(SPLIT, T))
        fetch(0, whole)
        add_turned(z[0], whole, True, False)
        add_turned(ys, whole, False, False)
        fetch(1, whole)
        add_turned(z[1], whole, False, False)
        partial = []
        for h, cols in enumerate(halves):
            fetch(2, cols)
            add_turned(z[2], cols, False, True)
            back = psum_s.tile([P, 512], F32, name="shared_bank%d" % h)
            partial.append(back)
            for i in range(cols.start // P, cols.stop // P):
                nc.scalar.copy(out=turned[:, blocks[i]], in_=sums[i][:, :P])
                nc.tensor.transpose(
                    back[:, i * P - cols.start : (i + 1) * P - cols.start], turned[:, blocks[i]], identity[:]
                )
        for cols in halves:
            fetch(3, cols)
        for h, cols in enumerate(halves):
            nc.vector.tensor_tensor(
                total[:, cols], partial[h][:, : cols.stop - cols.start], z[3][:, cols], ADD
            )
            nc.sync.dma_start(out=out[:, cols], in_=total[:, cols])
